import numpy as np, ml_dtypes
CORES = [24,26,29,31,48,50,53,55]
N = 8
WB, KB, QP = 2, 1, 128
def setup_inputs(rng):
    return {"q": rng.standard_normal((N, 128, QP), dtype=np.float32).astype(ml_dtypes.bfloat16), "k": rng.standard_normal((N, 128, KB * 128), dtype=np.float32).astype(ml_dtypes.bfloat16), "v": rng.standard_normal((N, 128, KB * 128), dtype=np.float32).astype(ml_dtypes.bfloat16)}
def setup_inputs_big(rng):
    d = setup_inputs(rng)
    for k in ("q", "k", "v"): d[k] = (d[k].astype(np.float32) * 1024.0).astype(d[k].dtype)
    return d
def setup_inputs_small(rng):
    d = setup_inputs(rng)
    for k in ("q", "k", "v"): d[k] = (d[k].astype(np.float32) * (1 / 1024.0)).astype(d[k].dtype)
    return d
def setup_inputs_apart(rng):
    d = setup_inputs(rng)
    f = (10.0 ** rng.permutation(np.linspace(-1.5, 1.5, N))).astype(np.float32).reshape(N, 1, 1)
    for k in ("q", "k", "v"): d[k] = (d[k].astype(np.float32) * f).astype(d[k].dtype)
    return d
def reference(q, k, v):
    Q, K, V = q.astype(np.float64), k.astype(np.float64), v.astype(np.float64)
    y = np.zeros((N, 128, QP))
    for r in range(N):
        for j in range(max(0, r - WB), r + 1):
            for b in range(KB):
                S = np.maximum(K[j][:, 128 * b:128 * b + 128].T @ Q[r], 0.0)
                y[r] += V[j][:, 128 * b:128 * b + 128].T @ S
    return {"y": y.astype(ml_dtypes.bfloat16 if q.dtype != np.float64 else np.float64)}

@@ -1,0 +1,139 @@
+from concourse.bass import DstId, RemoteDMATransfer
+from concourse.mybir import AluOpType
+
+WB = 2
+NS = WB + 1
+D = 128
+NE = 8
+
+SCRATCH = {
+    "kv0": ("sbuf", [D, 2 * D], "bfloat16"),
+    "kv1": ("sbuf", [D, 2 * D], "bfloat16"),
+    "kv2": ("sbuf", [D, 2 * D], "bfloat16"),
+    "relay": ("sbuf", [D, 2 * D], "bfloat16"),
+    "qs": ("sbuf", [D, D], "bfloat16"),
+    "zero": ("sbuf", [D, D], "float32"),
+    "s0": ("sbuf", [D, D], "bfloat16"),
+    "s1": ("sbuf", [D, D], "bfloat16"),
+    "s2": ("sbuf", [D, D], "bfloat16"),
+    "ys": ("sbuf", [D, D], "bfloat16"),
+    "ps0": ("psum", [D, 512], "float32"),
+    "ps1": ("psum", [D, 512], "float32"),
+    "ps2": ("psum", [D, 512], "float32"),
+    "po": ("psum", [D, 512], "float32"),
+}
+SEMAPHORES = ["ldkv", "ldq", "arr0", "arr1", "arr2", "rarr", "sent", "zs",
+              "mm0", "mm1", "mm2", "rl0", "rl1", "rl2", "oo", "cp", "st"]
+
+
+def _plan(cores, topo):
+    n = len(cores)
+    direct = {j: [] for j in range(n)}
+    hops = []
+    for j in range(n):
+        for r in range(j + 1, min(n, j + WB + 1)):
+            if topo.may_write(cores[j], cores[r]):
+                direct[j].append(r)
+            else:
+                hops.append((j, r))
+
+    def port(c):
+        return (topo.chip(c), topo.die(c))
+
+    load = {}
+    for j in range(n):
+        for r in direct[j]:
+            if topo.chip(cores[j]) != topo.chip(cores[r]):
+                load[port(cores[j])] = load.get(port(cores[j]), 0) + 1
+    relay = {}
+    for j, r in hops:
+        cands = [c for c in cores
+                 if c != cores[j] and topo.chip(c) == topo.chip(cores[j]) and topo.may_write(c, cores[r])
+                 and c not in relay.values()]
+        best = min(cands, key=lambda c: (load.get(port(c), 0), c))
+        load[port(best)] = load.get(port(best), 0) + 1
+        relay[(j, r)] = best
+    late = [r for (_j, r) in hops]
+    for j in range(n):
+        direct[j].sort(key=lambda r: (r in late, r))
+    return direct, relay
+
+
+def _pick(allowed, n):
+    bits = [b for b in range(allowed.bit_length()) if (allowed >> b) & 1]
+    return sum(1 << b for b in bits[::len(bits) // n][:n])
+
+
+def rank_program(g, core, T, topo):
+    rank = T.rank_of(core)
+    if rank is None:
+        return
+    cores = list(T.cores)
+    direct, relay = _plan(cores, topo)
+    sem = T.sem
+    own = T["kv%d" % (rank % NS)]
+
+    g.sync.dma_start(own[:, 0:D], T.k[:, :]).then_inc(sem.ldkv, 16)
+    g.scalar.dma_start(own[:, D:2 * D], T.v[:, :]).then_inc(sem.ldkv, 16)
+    g.sync.wait_ge(sem.ldkv, 32)
+    g.sync.dma_start(T.qs[:, :], T.q[:, :]).then_inc(sem.ldq, 16)
+
+    handed = [c for (j, _r), c in relay.items() if j == rank]
+    duty = [(j, r) for (j, r), c in relay.items() if c == core]
+    targets = handed + [cores[r] for r in direct[rank]] + [cores[r] for (_j, r) in duty]
+    if targets:
+        allowed = topo.mask(core, targets[0])
+        for d in targets[1:]:
+            allowed &= topo.mask(core, d)
+        eng = _pick(allowed, NE)
+        sent = 0
+        g.wait_ge(sem.ldkv, 32)
+        for c in handed:
+            rid, pid, _se = topo.addr(c)
+            g.remote_dma(out_ap=T.relay[:, :], in_ap=own[:, :], remote_sem=sem.rarr, local_sem=sem.sent,
+                         pid=pid, routing_id=rid, dma_engine_mask=eng)
+            sent += NE
+        if direct[rank]:
+            ids = []
+            for r in direct[rank]:
+                rid, pid, _se = topo.addr(cores[r])
+                ids.append(DstId(rid=rid, pnc=pid))
+            g.remote_dma_fused([RemoteDMATransfer(dst_ids=ids, dma_engine_mask=eng,
+                                                  remote_sem=sem["arr%d" % (rank % NS)],
+                                                  srcs=[own[:, :]], dsts=[own[:, :] for _i in ids], alu_op=0)],
+                               local_sem=sem.sent)
+            sent += NE
+        for j, r in duty:
+            rid, pid, _se = topo.addr(cores[r])
+            g.wait_ge(sem.rarr, NE)
+            g.remote_dma(out_ap=T["kv%d" % (j % NS)][:, :], in_ap=T.relay[:, :],
+                         remote_sem=sem["arr%d" % (j % NS)], local_sem=sem.sent,
+                         pid=pid, routing_id=rid, dma_engine_mask=eng)
+            sent += NE
+        g.wait_ge(sem.sent, sent)
+
+    js = [j for j in range(rank, rank - NS, -1) if j >= 0]
+    last = len(js) - 1
+    g.vector.memset(T.zero[:, :], 0.0).then_inc(sem.zs, 1)
+    g.vector.wait_ge(sem.zs, 1)
+    for i, j in enumerate(js):
+        blk = T["kv%d" % (j % NS)]
+        ps = T["ps%d" % i]
+        sb = T["s%d" % i]
+        if i == 0:
+            g.tensor.wait_ge(sem.ldkv, 32)
+            g.tensor.wait_ge(sem.ldq, 16)
+        else:
+            g.tensor.wait_ge(sem["arr%d" % (j % NS)], NE)
+        g.tensor.matmul(ps[:, 0:D], blk[:, 0:D], T.qs[:, :], start=True, stop=True).then_inc(sem["mm%d" % i], 1)
+        g.vector.wait_ge(sem["mm%d" % i], 1)
+        g.vector.tensor_tensor(sb[:, :], ps[:, 0:D], T.zero[:, :], AluOpType.max).then_inc(sem["rl%d" % i], 1)
+        g.tensor.wait_ge(sem["rl%d" % i], 1)
+        mm = g.tensor.matmul(T.po[:, 0:D], blk[:, D:2 * D], sb[:, :], start=(i == 0), stop=(i == last))
+        if i == last:
+            mm.then_inc(sem.oo, 1)
+    g.vector.wait_ge(sem.oo, 1)
+    g.vector.tensor_copy(T.ys[:, :], T.po[:, 0:D]).then_inc(sem.cp, 1)
+    g.sync.wait_ge(sem.cp, 1)
+    g.sync.dma_start(T.y[:, :], T.ys[:, :]).then_inc(sem.st, 16)
+    g.sync.wait_ge(sem.st, 16)

@@ -1,67 +1,157 @@
 from concourse.bass import DstId, RemoteDMATransfer
-from concourse.mybir import AluOpType
+from concourse.mybir import AluOpType, ActivationFunctionType
 
 WB = 2
 NS = WB + 1
 D = 128
-NE = 8
+W = 2 * D
+H = D // 2
+NH = 8
+NX = 8
+NN = 8
+NF = 16
 
 SCRATCH = {
-    "kv0": ("sbuf", [D, 2 * D], "bfloat16"),
-    "kv1": ("sbuf", [D, 2 * D], "bfloat16"),
-    "kv2": ("sbuf", [D, 2 * D], "bfloat16"),
-    "relay": ("sbuf", [D, 2 * D], "bfloat16"),
+    "kv0": ("sbuf", [D, W], "bfloat16"),
+    "kv1": ("sbuf", [D, W], "bfloat16"),
+    "kv2": ("sbuf", [D, W], "bfloat16"),
+    "hk": ("dram", [D, D], "bfloat16"),
+    "hv": ("dram", [D, D], "bfloat16"),
     "qs": ("sbuf", [D, D], "bfloat16"),
-    "zero": ("sbuf", [D, D], "float32"),
     "s0": ("sbuf", [D, D], "bfloat16"),
     "s1": ("sbuf", [D, D], "bfloat16"),
     "s2": ("sbuf", [D, D], "bfloat16"),
     "ys": ("sbuf", [D, D], "bfloat16"),
-    "ps0": ("psum", [D, 512], "float32"),
-    "ps1": ("psum", [D, 512], "float32"),
-    "ps2": ("psum", [D, 512], "float32"),
-    "po": ("psum", [D, 512], "float32"),
+    "pa0": ("psum", [D, 512], "float32"),
+    "pa1": ("psum", [D, 512], "float32"),
+    "pa2": ("psum", [D, 512], "float32"),
+    "pb0": ("psum", [D, 512], "float32"),
+    "pb1": ("psum", [D, 512], "float32"),
+    "pb2": ("psum", [D, 512], "float32"),
+    "oa": ("psum", [D, 512], "float32"),
+    "ob": ("psum", [D, 512], "float32"),
 }
-SEMAPHORES = ["ldkv", "ldq", "arr0", "arr1", "arr2", "rarr", "sent", "zs",
-              "mm0", "mm1", "mm2", "rl0", "rl1", "rl2", "oo", "cp", "st"]
+SEMAPHORES = ["ldkv", "ldown", "ldq", "arr0", "arr1", "arr2", "rarr", "sent",
+              "ma0", "ma1", "ma2", "mb0", "mb1", "mb2", "ra0", "ra1", "ra2", "rb0", "rb1", "rb2",
+              "fa", "fb", "cp", "st"]
+
+
+def _bits(m):
+    return [b for b in range(m.bit_length()) if (m >> b) & 1]
+
+
+def _mask(bits):
+    return sum(1 << b for b in bits)
+
+
+def _pick(allowed, n):
+    bits = _bits(allowed)
+    return _mask(bits[::len(bits) // n][:n])
 
 
 def _plan(cores, topo):
     n = len(cores)
-    direct = {j: [] for j in range(n)}
-    hops = []
+    near, cross, fwd = {}, {}, {}
     for j in range(n):
-        for r in range(j + 1, min(n, j + WB + 1)):
-            if topo.may_write(cores[j], cores[r]):
-                direct[j].append(r)
-            else:
-                hops.append((j, r))
+        rs = list(range(j + 1, min(n, j + WB + 1)))
+        near[j] = [r for r in rs if topo.chip(cores[r]) == topo.chip(cores[j])]
+        far = {}
+        for r in rs:
+            if r not in near[j]:
+                far.setdefault(topo.chip(cores[r]), []).append(r)
+        cross[j] = [grp[0] for grp in far.values()]
+        fwd[j] = [(grp[0], grp[1:]) for grp in far.values() if grp[1:]]
 
     def port(c):
         return (topo.chip(c), topo.die(c))
 
     load = {}
+    hops = []
     for j in range(n):
-        for r in direct[j]:
-            if topo.chip(cores[j]) != topo.chip(cores[r]):
-                load[port(cores[j])] = load.get(port(cores[j]), 0) + 1
+        for r in cross[j]:
+            if topo.may_write(cores[j], cores[r]):
+                load[port(cores[j])] = load.get(port(cores[j]), 0) + 2
+            else:
+                hops.append((j, r))
     relay = {}
     for j, r in hops:
         cands = [c for c in cores
-                 if c != cores[j] and topo.chip(c) == topo.chip(cores[j]) and topo.may_write(c, cores[r])
-                 and c not in relay.values()]
-        best = min(cands, key=lambda c: (load.get(port(c), 0), c))
-        load[port(best)] = load.get(port(best), 0) + 1
-        relay[(j, r)] = best
-    late = [r for (_j, r) in hops]
+                 if c != cores[j] and topo.chip(c) == topo.chip(cores[j]) and topo.may_write(c, cores[r])]
+        cands.sort(key=lambda c: (load.get(port(c), 0), c))
+        pair = [cands[0], cands[1 % len(cands)]]
+        for c in pair:
+            load[port(c)] = load.get(port(c), 0) + 1
+        relay[(j, r)] = pair
+
+    calls = {c: [] for c in cores}
+    arrive = {}
+    late = {c: [] for c in cores}
+    staged = []
     for j in range(n):
-        direct[j].sort(key=lambda r: (r in late, r))
-    return direct, relay
-
-
-def _pick(allowed, n):
-    bits = [b for b in range(allowed.bit_length()) if (allowed >> b) & 1]
-    return sum(1 << b for b in bits[::len(bits) // n][:n])
+        c = cores[j]
+        kv = "kv%d" % (j % NS)
+        arr = "arr%d" % (j % NS)
+        passes_off = [r for (_j, r), pair in relay.items() if c in pair]
+        passes_on = [e for jj in range(n) for (e, _rest) in fwd[jj] if e == j]
+        used = 0
+        for r in cross[j]:
+            if (j, r) in relay:
+                xa, xb = relay[(j, r)]
+                bits = _bits(_pick(topo.mask(c, xa) & topo.mask(c, xb), NH))
+                ms = [_mask(bits[0::2]), _mask(bits[1::2])]
+                used |= ms[0] | ms[1]
+                staged.append(c)
+                calls[c].append((None, [("hk", 0, D, "hk", 0, D, [xa], "rarr", ms[0]),
+                                        ("hv", 0, D, "hv", 0, D, [xb], "rarr", ms[1])]))
+                got = len(bits) if xa == xb else len(bits) // 2
+                total = 0
+                for h, x in enumerate((xa, xb)):
+                    mo = _pick(topo.mask(x, cores[r]), NX)
+                    late[x].append((("rarr", got), [(("hk", "hv")[h], 0, D, kv, h * D, (h + 1) * D, [cores[r]], arr, mo)]))
+                    total += len(_bits(mo))
+                arrive[(j, cores[r])] = total
+            else:
+                m = _pick(topo.mask(c, cores[r]), NX)
+                used |= m
+                calls[c].append((None, [(kv, 0, W, kv, 0, W, [cores[r]], arr, m)]))
+                arrive[(j, cores[r])] = len(_bits(m))
+        if near[j]:
+            allowed = topo.mask(c, cores[near[j][0]])
+            for r in near[j][1:]:
+                allowed &= topo.mask(c, cores[r])
+            wait = ("ldown", 32) if c in staged else None
+            if passes_off:
+                out = allowed & topo.mask(c, cores[passes_off[0]])
+                sets = [_pick(out, NX), _pick(allowed & ~out, NX)]
+                for i, r in enumerate(near[j]):
+                    m = sets[i % 2]
+                    calls[c].append((wait, [(kv, 0, W, kv, 0, W, [cores[r]], arr, m)]))
+                    arrive[(j, cores[r])] = len(_bits(m))
+            else:
+                if passes_on:
+                    m = _pick(allowed, NF)
+                elif used:
+                    m = used
+                else:
+                    m = _pick(allowed, NN)
+                calls[c].append((wait, [(kv, 0, W, kv, 0, W, [cores[r] for r in near[j]], arr, m)]))
+                for r in near[j]:
+                    arrive[(j, cores[r])] = len(_bits(m))
+    for j in range(n):
+        kv = "kv%d" % (j % NS)
+        arr = "arr%d" % (j % NS)
+        for e, rest in fwd[j]:
+            x = cores[e]
+            m = topo.mask(x, cores[rest[0]])
+            for r in rest[1:]:
+                m &= topo.mask(x, cores[r])
+            m = _pick(m, NF)
+            late[x].append(((arr, arrive[(j, x)]), [(kv, 0, W, kv, 0, W, [cores[r] for r in rest], arr, m)]))
+            for r in rest:
+                arrive[(j, cores[r])] = len(_bits(m))
+    for c in cores:
+        calls[c] += late[c]
+    return calls, arrive, staged
 
 
 def rank_program(g, core, T, topo):
@@ -69,71 +159,72 @@ def rank_program(g, core, T, topo):
     if rank is None:
         return
     cores = list(T.cores)
-    direct, relay = _plan(cores, topo)
+    calls, arrive, staged_cores = _plan(cores, topo)
     sem = T.sem
     own = T["kv%d" % (rank % NS)]
+    staged = core in staged_cores
 
-    g.sync.dma_start(own[:, 0:D], T.k[:, :]).then_inc(sem.ldkv, 16)
-    g.scalar.dma_start(own[:, D:2 * D], T.v[:, :]).then_inc(sem.ldkv, 16)
-    g.sync.wait_ge(sem.ldkv, 32)
+    if staged:
+        g.sync.dma_start(T.hk[:, :], T.k[:, :]).then_inc(sem.ldkv, 16)
+        g.scalar.dma_start(T.hv[:, :], T.v[:, :]).then_inc(sem.ldkv, 16)
+        g.sync.wait_ge(sem.ldkv, 32)
+        g.scalar.wait_ge(sem.ldkv, 32)
+        g.sync.dma_start(own[:, 0:D], T.k[:, :]).then_inc(sem.ldown, 16)
+        g.scalar.dma_start(own[:, D:W], T.v[:, :]).then_inc(sem.ldown, 16)
+    else:
+        g.sync.dma_start(own[:, 0:D], T.k[:, :]).then_inc(sem.ldkv, 16)
+        g.scalar.dma_start(own[:, D:W], T.v[:, :]).then_inc(sem.ldkv, 16)
+        g.sync.wait_ge(sem.ldkv, 32)
     g.sync.dma_start(T.qs[:, :], T.q[:, :]).then_inc(sem.ldq, 16)
 
-    handed = [c for (j, _r), c in relay.items() if j == rank]
-    duty = [(j, r) for (j, r), c in relay.items() if c == core]
-    targets = handed + [cores[r] for r in direct[rank]] + [cores[r] for (_j, r) in duty]
-    if targets:
-        allowed = topo.mask(core, targets[0])
-        for d in targets[1:]:
-            allowed &= topo.mask(core, d)
-        eng = _pick(allowed, NE)
+    if calls[core]:
         sent = 0
         g.wait_ge(sem.ldkv, 32)
-        for c in handed:
-            rid, pid, _se = topo.addr(c)
-            g.remote_dma(out_ap=T.relay[:, :], in_ap=own[:, :], remote_sem=sem.rarr, local_sem=sem.sent,
-                         pid=pid, routing_id=rid, dma_engine_mask=eng)
-            sent += NE
-        if direct[rank]:
-            ids = []
-            for r in direct[rank]:
-                rid, pid, _se = topo.addr(cores[r])
-                ids.append(DstId(rid=rid, pnc=pid))
-            g.remote_dma_fused([RemoteDMATransfer(dst_ids=ids, dma_engine_mask=eng,
-                                                  remote_sem=sem["arr%d" % (rank % NS)],
-                                                  srcs=[own[:, :]], dsts=[own[:, :] for _i in ids], alu_op=0)],
-                               local_sem=sem.sent)
-            sent += NE
-        for j, r in duty:
-            rid, pid, _se = topo.addr(cores[r])
-            g.wait_ge(sem.rarr, NE)
-            g.remote_dma(out_ap=T["kv%d" % (j % NS)][:, :], in_ap=T.relay[:, :],
-                         remote_sem=sem["arr%d" % (j % NS)], local_sem=sem.sent,
-                         pid=pid, routing_id=rid, dma_engine_mask=eng)
-            sent += NE
+        for wait, transfers in calls[core]:
+            if wait is not None:
+                g.wait_ge(sem[wait[0]], wait[1])
+            trs = []
+            for src, slo, shi, dst, dlo, dhi, dests, landing, m in transfers:
+                ids = []
+                for d in dests:
+                    rid, pid, _se = topo.addr(d)
+                    ids.append(DstId(rid=rid, pnc=pid))
+                trs.append(RemoteDMATransfer(dst_ids=ids, dma_engine_mask=m, remote_sem=sem[landing],
+                                             srcs=[T[src][:, slo:shi]], dsts=[T[dst][:, dlo:dhi] for _i in ids],
+                                             alu_op=0))
+                sent += len(_bits(m))
+            g.remote_dma_fused(trs, local_sem=sem.sent)
         g.wait_ge(sem.sent, sent)
 
     js = [j for j in range(rank, rank - NS, -1) if j >= 0]
     last = len(js) - 1
-    g.vector.memset(T.zero[:, :], 0.0).then_inc(sem.zs, 1)
-    g.vector.wait_ge(sem.zs, 1)
     for i, j in enumerate(js):
         blk = T["kv%d" % (j % NS)]
-        ps = T["ps%d" % i]
-        sb = T["s%d" % i]
+        pa, pb, sb = T["pa%d" % i], T["pb%d" % i], T["s%d" % i]
         if i == 0:
             g.tensor.wait_ge(sem.ldkv, 32)
+            if staged:
+                g.tensor.wait_ge(sem.ldown, 32)
             g.tensor.wait_ge(sem.ldq, 16)
         else:
-            g.tensor.wait_ge(sem["arr%d" % (j % NS)], NE)
-        g.tensor.matmul(ps[:, 0:D], blk[:, 0:D], T.qs[:, :], start=True, stop=True).then_inc(sem["mm%d" % i], 1)
-        g.vector.wait_ge(sem["mm%d" % i], 1)
-        g.vector.tensor_tensor(sb[:, :], ps[:, 0:D], T.zero[:, :], AluOpType.max).then_inc(sem["rl%d" % i], 1)
-        g.tensor.wait_ge(sem["rl%d" % i], 1)
-        mm = g.tensor.matmul(T.po[:, 0:D], blk[:, D:2 * D], sb[:, :], start=(i == 0), stop=(i == last))
+            g.tensor.wait_ge(sem["arr%d" % (j % NS)], arrive[(j, core)])
+        g.tensor.matmul(pa[:, 0:H], blk[:, 0:D], T.qs[:, 0:H], start=True, stop=True).then_inc(sem["ma%d" % i], 1)
+        g.tensor.matmul(pb[:, 0:H], blk[:, 0:D], T.qs[:, H:D], start=True, stop=True).then_inc(sem["mb%d" % i], 1)
+        g.vector.wait_ge(sem["ma%d" % i], 1)
+        g.vector.tensor_scalar(sb[:, 0:H], pa[:, 0:H], 0.0, None, AluOpType.max).then_inc(sem["ra%d" % i], 1)
+        g.scalar.wait_ge(sem["mb%d" % i], 1)
+        g.scalar.activation(sb[:, H:D], pb[:, 0:H], ActivationFunctionType.Relu).then_inc(sem["rb%d" % i], 1)
+        g.tensor.wait_ge(sem["ra%d" % i], 1)
+        ma = g.tensor.matmul(T.oa[:, 0:H], blk[:, D:W], sb[:, 0:H], start=(i == 0), stop=(i == last))
+        g.tensor.wait_ge(sem["rb%d" % i], 1)
+        mb = g.tensor.matmul(T.ob[:, 0:H], blk[:, D:W], sb[:, H:D], start=(i == 0), stop=(i == last))
         if i == last:
-            mm.then_inc(sem.oo, 1)
-    g.vector.wait_ge(sem.oo, 1)
-    g.vector.tensor_copy(T.ys[:, :], T.po[:, 0:D]).then_inc(sem.cp, 1)
-    g.sync.wait_ge(sem.cp, 1)
+            ma.then_inc(sem.fa, 1)
+            mb.then_inc(sem.fb, 1)
+    g.vector.wait_ge(sem.fa, 1)
+    g.vector.tensor_copy(T.ys[:, 0:H], T.oa[:, 0:H]).then_inc(sem.cp, 1)
+    g.scalar.wait_ge(sem.fb, 1)
+    g.scalar.activation(T.ys[:, H:D], T.ob[:, 0:H], ActivationFunctionType.Copy).then_inc(sem.cp, 1)
+    g.sync.wait_ge(sem.cp, 2)
     g.sync.dma_start(T.y[:, :], T.ys[:, :]).then_inc(sem.st, 16)
     g.sync.wait_ge(sem.st, 16)

@@ -15,6 +15,8 @@ SCRATCH = {
     "kv0": ("sbuf", [D, W], "bfloat16"),
     "kv1": ("sbuf", [D, W], "bfloat16"),
     "kv2": ("sbuf", [D, W], "bfloat16"),
+    "ok": ("dram", [D, D], "bfloat16"),
+    "ov": ("dram", [D, D], "bfloat16"),
     "hk": ("dram", [D, D], "bfloat16"),
     "hv": ("dram", [D, D], "bfloat16"),
     "qs": ("sbuf", [D, D], "bfloat16"),
@@ -31,9 +33,12 @@ SCRATCH = {
     "oa": ("psum", [D, 512], "float32"),
     "ob": ("psum", [D, 512], "float32"),
 }
-SEMAPHORES = ["ldkv", "ldown", "ldq", "arr0", "arr1", "arr2", "rarr", "sent",
+SEMAPHORES = ["ldk", "ldv", "ldown", "ldq", "arr0", "arr1", "arr2", "vrr0", "vrr1", "vrr2", "rarr", "sent",
               "ma0", "ma1", "ma2", "mb0", "mb1", "mb2", "ra0", "ra1", "ra2", "rb0", "rb1", "rb2",
               "fa", "fb", "cp", "st"]
+OWN = ("ok", "ov")
+LAND = ("hk", "hv")
+LD = (("ldk", 16), ("ldv", 16))
 
 
 def _bits(m):
@@ -49,18 +54,24 @@ def _pick(allowed, n):
     return _mask(bits[::len(bits) // n][:n])
 
 
+def _common(topo, c, dests):
+    m = topo.mask(c, dests[0])
+    for d in dests[1:]:
+        m &= topo.mask(c, d)
+    return m
+
+
 def _plan(cores, topo):
     n = len(cores)
-    near, cross, fwd = {}, {}, {}
+    near, far = {}, {}
     for j in range(n):
         rs = list(range(j + 1, min(n, j + WB + 1)))
         near[j] = [r for r in rs if topo.chip(cores[r]) == topo.chip(cores[j])]
-        far = {}
+        grps = {}
         for r in rs:
             if r not in near[j]:
-                far.setdefault(topo.chip(cores[r]), []).append(r)
-        cross[j] = [grp[0] for grp in far.values()]
-        fwd[j] = [(grp[0], grp[1:]) for grp in far.values() if grp[1:]]
+                grps.setdefault(topo.chip(cores[r]), []).append(r)
+        far[j] = list(grps.values())
 
     def port(c):
         return (topo.chip(c), topo.die(c))
@@ -68,11 +79,11 @@ def _plan(cores, topo):
     load = {}
     hops = []
     for j in range(n):
-        for r in cross[j]:
-            if topo.may_write(cores[j], cores[r]):
+        for grp in far[j]:
+            if topo.may_write(cores[j], cores[grp[0]]):
                 load[port(cores[j])] = load.get(port(cores[j]), 0) + 2
             else:
-                hops.append((j, r))
+                hops.append((j, grp[0]))
     relay = {}
     for j, r in hops:
         cands = [c for c in cores
@@ -82,76 +93,71 @@ def _plan(cores, topo):
         for c in pair:
             load[port(c)] = load.get(port(c), 0) + 1
         relay[(j, r)] = pair
+    inside = [grp[0] for j in range(n) for grp in far[j] if grp[1:]]
 
     calls = {c: [] for c in cores}
-    arrive = {}
     late = {c: [] for c in cores}
-    staged = []
+    arrive = {}
+    staged, halves = [], []
     for j in range(n):
         c = cores[j]
         kv = "kv%d" % (j % NS)
-        arr = "arr%d" % (j % NS)
+        lands = ("arr%d" % (j % NS), "vrr%d" % (j % NS))
         passes_off = [r for (_j, r), pair in relay.items() if c in pair]
-        passes_on = [e for jj in range(n) for (e, _rest) in fwd[jj] if e == j]
         used = 0
-        for r in cross[j]:
-            if (j, r) in relay:
-                xa, xb = relay[(j, r)]
-                bits = _bits(_pick(topo.mask(c, xa) & topo.mask(c, xb), NH))
+        for grp in far[j]:
+            x = cores[grp[0]]
+            rest = [cores[t] for t in grp[1:]]
+            halves.append(c)
+            arrive[(j, x)] = [0, 0]
+            if (j, grp[0]) in relay:
+                pair = relay[(j, grp[0])]
+                bits = _bits(_pick(_common(topo, c, pair), NH))
                 ms = [_mask(bits[0::2]), _mask(bits[1::2])]
-                used |= ms[0] | ms[1]
                 staged.append(c)
-                calls[c].append((None, [("hk", 0, D, "hk", 0, D, [xa], "rarr", ms[0]),
-                                        ("hv", 0, D, "hv", 0, D, [xb], "rarr", ms[1])]))
-                got = len(bits) if xa == xb else len(bits) // 2
-                total = 0
-                for h, x in enumerate((xa, xb)):
-                    mo = _pick(topo.mask(x, cores[r]), NX)
-                    late[x].append((("rarr", got), [(("hk", "hv")[h], 0, D, kv, h * D, (h + 1) * D, [cores[r]], arr, mo)]))
-                    total += len(_bits(mo))
-                arrive[(j, cores[r])] = total
+                for h, p in enumerate(pair):
+                    used |= ms[h]
+                    calls[c].append(([LD[h]], [(OWN[h], 0, D, LAND[h], 0, D, [p], "rarr", ms[h])]))
+                    got = len(_bits(ms[h])) * (h + 1 if pair[0] == pair[1] else 1)
+                    mo = _pick(topo.mask(p, x), NX)
+                    late[p].append(([("rarr", got)], [(LAND[h], 0, D, kv, h * D, (h + 1) * D, [x], lands[h], mo)]))
+                    arrive[(j, x)][h] = len(_bits(mo))
             else:
-                m = _pick(topo.mask(c, cores[r]), NX)
+                m = _pick(topo.mask(c, x), NX)
                 used |= m
-                calls[c].append((None, [(kv, 0, W, kv, 0, W, [cores[r]], arr, m)]))
-                arrive[(j, cores[r])] = len(_bits(m))
+                for h in range(2):
+                    calls[c].append(([LD[h]], [(kv, h * D, (h + 1) * D, kv, h * D, (h + 1) * D, [x], lands[h], m)]))
+                    arrive[(j, x)][h] = len(_bits(m))
+            if rest:
+                mf = _pick(_common(topo, x, rest), NF)
+                for h in range(2):
+                    late[x].append(([(lands[h], arrive[(j, x)][h])],
+                                    [(kv, h * D, (h + 1) * D, kv, h * D, (h + 1) * D, rest, lands[h], mf)]))
+                for t in rest:
+                    arrive[(j, t)] = [len(_bits(mf)), len(_bits(mf))]
         if near[j]:
-            allowed = topo.mask(c, cores[near[j][0]])
-            for r in near[j][1:]:
-                allowed &= topo.mask(c, cores[r])
-            wait = ("ldown", 32) if c in staged else None
+            allowed = _common(topo, c, [cores[r] for r in near[j]])
+            wait = [("ldown", 32)] if c in staged else list(LD)
             if passes_off:
                 out = allowed & topo.mask(c, cores[passes_off[0]])
                 sets = [_pick(out, NX), _pick(allowed & ~out, NX)]
                 for i, r in enumerate(near[j]):
                     m = sets[i % 2]
-                    calls[c].append((wait, [(kv, 0, W, kv, 0, W, [cores[r]], arr, m)]))
-                    arrive[(j, cores[r])] = len(_bits(m))
+                    calls[c].append((wait, [(kv, 0, W, kv, 0, W, [cores[r]], lands[0], m)]))
+                    arrive[(j, cores[r])] = [len(_bits(m)), 0]
             else:
-                if passes_on:
+                if j in inside:
                     m = _pick(allowed, NF)
                 elif used:
                     m = used
                 else:
                     m = _pick(allowed, NN)
-                calls[c].append((wait, [(kv, 0, W, kv, 0, W, [cores[r] for r in near[j]], arr, m)]))
+                calls[c].append((wait, [(kv, 0, W, kv, 0, W, [cores[r] for r in near[j]], lands[0], m)]))
                 for r in near[j]:
-                    arrive[(j, cores[r])] = len(_bits(m))
-    for j in range(n):
-        kv = "kv%d" % (j % NS)
-        arr = "arr%d" % (j % NS)
-        for e, rest in fwd[j]:
-            x = cores[e]
-            m = topo.mask(x, cores[rest[0]])
-            for r in rest[1:]:
-                m &= topo.mask(x, cores[r])
-            m = _pick(m, NF)
-            late[x].append(((arr, arrive[(j, x)]), [(kv, 0, W, kv, 0, W, [cores[r] for r in rest], arr, m)]))
-            for r in rest:
-                arrive[(j, cores[r])] = len(_bits(m))
+                    arrive[(j, cores[r])] = [len(_bits(m)), 0]
     for c in cores:
         calls[c] += late[c]
-    return calls, arrive, staged
+    return calls, arrive, staged, halves
 
 
 def rank_program(g, core, T, topo):
@@ -159,30 +165,32 @@ def rank_program(g, core, T, topo):
     if rank is None:
         return
     cores = list(T.cores)
-    calls, arrive, staged_cores = _plan(cores, topo)
+    calls, arrive, staged_cores, halves = _plan(cores, topo)
     sem = T.sem
     own = T["kv%d" % (rank % NS)]
     staged = core in staged_cores
 
+    vq = g.sync if core in halves else g.scalar
     if staged:
-        g.sync.dma_start(T.hk[:, :], T.k[:, :]).then_inc(sem.ldkv, 16)
-        g.scalar.dma_start(T.hv[:, :], T.v[:, :]).then_inc(sem.ldkv, 16)
-        g.sync.wait_ge(sem.ldkv, 32)
-        g.scalar.wait_ge(sem.ldkv, 32)
+        g.sync.dma_start(T.ok[:, :], T.k[:, :]).then_inc(sem.ldk, 16)
+        vq.dma_start(T.ov[:, :], T.v[:, :]).then_inc(sem.ldv, 16)
+        for q in (g.sync, g.scalar):
+            q.wait_ge(sem.ldk, 16)
+            q.wait_ge(sem.ldv, 16)
         g.sync.dma_start(own[:, 0:D], T.k[:, :]).then_inc(sem.ldown, 16)
         g.scalar.dma_start(own[:, D:W], T.v[:, :]).then_inc(sem.ldown, 16)
     else:
-        g.sync.dma_start(own[:, 0:D], T.k[:, :]).then_inc(sem.ldkv, 16)
-        g.scalar.dma_start(own[:, D:W], T.v[:, :]).then_inc(sem.ldkv, 16)
-        g.sync.wait_ge(sem.ldkv, 32)
+        g.sync.dma_start(own[:, 0:D], T.k[:, :]).then_inc(sem.ldk, 16)
+        vq.dma_start(own[:, D:W], T.v[:, :]).then_inc(sem.ldv, 16)
+        g.sync.wait_ge(sem.ldk, 16)
+        g.sync.wait_ge(sem.ldv, 16)
     g.sync.dma_start(T.qs[:, :], T.q[:, :]).then_inc(sem.ldq, 16)
 
     if calls[core]:
         sent = 0
-        g.wait_ge(sem.ldkv, 32)
-        for wait, transfers in calls[core]:
-            if wait is not None:
-                g.wait_ge(sem[wait[0]], wait[1])
+        for waits, transfers in calls[core]:
+            for name, count in waits:
+                g.wait_ge(sem[name], count)
             trs = []
             for src, slo, shi, dst, dlo, dhi, dests, landing, m in transfers:
                 ids = []
@@ -201,19 +209,24 @@ def rank_program(g, core, T, topo):
     for i, j in enumerate(js):
         blk = T["kv%d" % (j % NS)]
         pa, pb, sb = T["pa%d" % i], T["pb%d" % i], T["s%d" % i]
+        need_v = 0
         if i == 0:
-            g.tensor.wait_ge(sem.ldkv, 32)
+            g.tensor.wait_ge(sem.ldk, 16)
+            g.tensor.wait_ge(sem.ldv, 16)
             if staged:
                 g.tensor.wait_ge(sem.ldown, 32)
             g.tensor.wait_ge(sem.ldq, 16)
         else:
-            g.tensor.wait_ge(sem["arr%d" % (j % NS)], arrive[(j, core)])
+            g.tensor.wait_ge(sem["arr%d" % (j % NS)], arrive[(j, core)][0])
+            need_v = arrive[(j, core)][1]
         g.tensor.matmul(pa[:, 0:H], blk[:, 0:D], T.qs[:, 0:H], start=True, stop=True).then_inc(sem["ma%d" % i], 1)
         g.tensor.matmul(pb[:, 0:H], blk[:, 0:D], T.qs[:, H:D], start=True, stop=True).then_inc(sem["mb%d" % i], 1)
         g.vector.wait_ge(sem["ma%d" % i], 1)
         g.vector.tensor_scalar(sb[:, 0:H], pa[:, 0:H], 0.0, None, AluOpType.max).then_inc(sem["ra%d" % i], 1)
         g.scalar.wait_ge(sem["mb%d" % i], 1)
         g.scalar.activation(sb[:, H:D], pb[:, 0:H], ActivationFunctionType.Relu).then_inc(sem["rb%d" % i], 1)
+        if need_v:
+            g.tensor.wait_ge(sem["vrr%d" % (j % NS)], need_v)
         g.tensor.wait_ge(sem["ra%d" % i], 1)
         ma = g.tensor.matmul(T.oa[:, 0:H], blk[:, D:W], sb[:, 0:H], start=(i == 0), stop=(i == last))
         g.tensor.wait_ge(sem["rb%d" % i], 1)

from concourse.bass import DstId, RemoteDMATransfer
from concourse.mybir import AluOpType, ActivationFunctionType

WB = 2
NS = WB + 1
D = 128
W = 2 * D
H = D // 2
NH = 8
NX = 8
NN = 8
NF = 16

SCRATCH = {
    "kv0": ("sbuf", [D, W], "bfloat16"),
    "kv1": ("sbuf", [D, W], "bfloat16"),
    "kv2": ("sbuf", [D, W], "bfloat16"),
    "ok": ("dram", [D, D], "bfloat16"),
    "ov": ("dram", [D, D], "bfloat16"),
    "hk": ("dram", [D, D], "bfloat16"),
    "hv": ("dram", [D, D], "bfloat16"),
    "qs": ("sbuf", [D, D], "bfloat16"),
    "s0": ("sbuf", [D, D], "bfloat16"),
    "s1": ("sbuf", [D, D], "bfloat16"),
    "s2": ("sbuf", [D, D], "bfloat16"),
    "ys": ("sbuf", [D, D], "bfloat16"),
    "pa0": ("psum", [D, 512], "float32"),
    "pa1": ("psum", [D, 512], "float32"),
    "pa2": ("psum", [D, 512], "float32"),
    "pb0": ("psum", [D, 512], "float32"),
    "pb1": ("psum", [D, 512], "float32"),
    "pb2": ("psum", [D, 512], "float32"),
    "oa": ("psum", [D, 512], "float32"),
    "ob": ("psum", [D, 512], "float32"),
}
SEMAPHORES = ["ldk", "ldv", "ldown", "ldq", "arr0", "arr1", "arr2", "vrr0", "vrr1", "vrr2", "rarr", "sent",
              "ma0", "ma1", "ma2", "mb0", "mb1", "mb2", "ra0", "ra1", "ra2", "rb0", "rb1", "rb2",
              "fa", "fb", "cp", "st"]
OWN = ("ok", "ov")
LAND = ("hk", "hv")
LD = (("ldk", 16), ("ldv", 16))


def _bits(m):
    return [b for b in range(m.bit_length()) if (m >> b) & 1]


def _mask(bits):
    return sum(1 << b for b in bits)


def _pick(allowed, n):
    bits = _bits(allowed)
    return _mask(bits[::len(bits) // n][:n])


def _common(topo, c, dests):
    m = topo.mask(c, dests[0])
    for d in dests[1:]:
        m &= topo.mask(c, d)
    return m


def _plan(cores, topo):
    n = len(cores)
    near, far = {}, {}
    for j in range(n):
        rs = list(range(j + 1, min(n, j + WB + 1)))
        near[j] = [r for r in rs if topo.chip(cores[r]) == topo.chip(cores[j])]
        grps = {}
        for r in rs:
            if r not in near[j]:
                grps.setdefault(topo.chip(cores[r]), []).append(r)
        far[j] = list(grps.values())

    def port(c):
        return (topo.chip(c), topo.die(c))

    load = {}
    hops = []
    for j in range(n):
        for grp in far[j]:
            if topo.may_write(cores[j], cores[grp[0]]):
                load[port(cores[j])] = load.get(port(cores[j]), 0) + 2
            else:
                hops.append((j, grp[0]))
    relay = {}
    for j, r in hops:
        cands = [c for c in cores
                 if c != cores[j] and topo.chip(c) == topo.chip(cores[j]) and topo.may_write(c, cores[r])]
        cands.sort(key=lambda c: (load.get(port(c), 0), c))
        pair = [cands[0], cands[1 % len(cands)]]
        for c in pair:
            load[port(c)] = load.get(port(c), 0) + 1
        relay[(j, r)] = pair
    inside = [grp[0] for j in range(n) for grp in far[j] if grp[1:]]

    calls = {c: [] for c in cores}
    late = {c: [] for c in cores}
    arrive = {}
    staged, halves = [], []
    for j in range(n):
        c = cores[j]
        kv = "kv%d" % (j % NS)
        lands = ("arr%d" % (j % NS), "vrr%d" % (j % NS))
        passes_off = [r for (_j, r), pair in relay.items() if c in pair]
        used = 0
        for grp in far[j]:
            x = cores[grp[0]]
            rest = [cores[t] for t in grp[1:]]
            halves.append(c)
            arrive[(j, x)] = [0, 0]
            if (j, grp[0]) in relay:
                pair = relay[(j, grp[0])]
                bits = _bits(_pick(_common(topo, c, pair), NH))
                ms = [_mask(bits[0::2]), _mask(bits[1::2])]
                staged.append(c)
                for h, p in enumerate(pair):
                    used |= ms[h]
                    calls[c].append(([LD[h]], [(OWN[h], 0, D, LAND[h], 0, D, [p], "rarr", ms[h])]))
                    got = len(_bits(ms[h])) * (h + 1 if pair[0] == pair[1] else 1)
                    mo = _pick(topo.mask(p, x), NX)
                    late[p].append(([("rarr", got)], [(LAND[h], 0, D, kv, h * D, (h + 1) * D, [x], lands[h], mo)]))
                    arrive[(j, x)][h] = len(_bits(mo))
            else:
                m = _pick(topo.mask(c, x), NX)
                used |= m
                for h in range(2):
                    calls[c].append(([LD[h]], [(kv, h * D, (h + 1) * D, kv, h * D, (h + 1) * D, [x], lands[h], m)]))
                    arrive[(j, x)][h] = len(_bits(m))
            if rest:
                mf = _pick(_common(topo, x, rest), NF)
                for h in range(2):
                    late[x].append(([(lands[h], arrive[(j, x)][h])],
                                    [(kv, h * D, (h + 1) * D, kv, h * D, (h + 1) * D, rest, lands[h], mf)]))
                for t in rest:
                    arrive[(j, t)] = [len(_bits(mf)), len(_bits(mf))]
        if near[j]:
            allowed = _common(topo, c, [cores[r] for r in near[j]])
            wait = [("ldown", 32)] if c in staged else list(LD)
            if passes_off:
                out = allowed & topo.mask(c, cores[passes_off[0]])
                sets = [_pick(out, NX), _pick(allowed & ~out, NX)]
                for i, r in enumerate(near[j]):
                    m = sets[i % 2]
                    calls[c].append((wait, [(kv, 0, W, kv, 0, W, [cores[r]], lands[0], m)]))
                    arrive[(j, cores[r])] = [len(_bits(m)), 0]
            else:
                if j in inside:
                    m = _pick(allowed, NF)
                elif used:
                    m = used
                else:
                    m = _pick(allowed, NN)
                calls[c].append((wait, [(kv, 0, W, kv, 0, W, [cores[r] for r in near[j]], lands[0], m)]))
                for r in near[j]:
                    arrive[(j, cores[r])] = [len(_bits(m)), 0]
    for c in cores:
        calls[c] += late[c]
    return calls, arrive, staged, halves


def rank_program(g, core, T, topo):
    rank = T.rank_of(core)
    if rank is None:
        return
    cores = list(T.cores)
    calls, arrive, staged_cores, halves = _plan(cores, topo)
    sem = T.sem
    own = T["kv%d" % (rank % NS)]
    staged = core in staged_cores

    vq = g.sync if core in halves else g.scalar
    if staged:
        g.sync.dma_start(T.ok[:, :], T.k[:, :]).then_inc(sem.ldk, 16)
        vq.dma_start(T.ov[:, :], T.v[:, :]).then_inc(sem.ldv, 16)
        for q in (g.sync, g.scalar):
            q.wait_ge(sem.ldk, 16)
            q.wait_ge(sem.ldv, 16)
        g.sync.dma_start(own[:, 0:D], T.k[:, :]).then_inc(sem.ldown, 16)
        g.scalar.dma_start(own[:, D:W], T.v[:, :]).then_inc(sem.ldown, 16)
    else:
        g.sync.dma_start(own[:, 0:D], T.k[:, :]).then_inc(sem.ldk, 16)
        vq.dma_start(own[:, D:W], T.v[:, :]).then_inc(sem.ldv, 16)
        g.sync.wait_ge(sem.ldk, 16)
        g.sync.wait_ge(sem.ldv, 16)
    g.sync.dma_start(T.qs[:, :], T.q[:, :]).then_inc(sem.ldq, 16)

    if calls[core]:
        sent = 0
        for waits, transfers in calls[core]:
            for name, count in waits:
                g.wait_ge(sem[name], count)
            trs = []
            for src, slo, shi, dst, dlo, dhi, dests, landing, m in transfers:
                ids = []
                for d in dests:
                    rid, pid, _se = topo.addr(d)
                    ids.append(DstId(rid=rid, pnc=pid))
                trs.append(RemoteDMATransfer(dst_ids=ids, dma_engine_mask=m, remote_sem=sem[landing],
                                             srcs=[T[src][:, slo:shi]], dsts=[T[dst][:, dlo:dhi] for _i in ids],
                                             alu_op=0))
                sent += len(_bits(m))
            g.remote_dma_fused(trs, local_sem=sem.sent)
        g.wait_ge(sem.sent, sent)

    js = [j for j in range(rank, rank - NS, -1) if j >= 0]
    last = len(js) - 1
    for i, j in enumerate(js):
        blk = T["kv%d" % (j % NS)]
        pa, pb, sb = T["pa%d" % i], T["pb%d" % i], T["s%d" % i]
        need_v = 0
        if i == 0:
            g.tensor.wait_ge(sem.ldk, 16)
            g.tensor.wait_ge(sem.ldv, 16)
            if staged:
                g.tensor.wait_ge(sem.ldown, 32)
            g.tensor.wait_ge(sem.ldq, 16)
        else:
            g.tensor.wait_ge(sem["arr%d" % (j % NS)], arrive[(j, core)][0])
            need_v = arrive[(j, core)][1]
        g.tensor.matmul(pa[:, 0:H], blk[:, 0:D], T.qs[:, 0:H], start=True, stop=True).then_inc(sem["ma%d" % i], 1)
        g.tensor.matmul(pb[:, 0:H], blk[:, 0:D], T.qs[:, H:D], start=True, stop=True).then_inc(sem["mb%d" % i], 1)
        g.vector.wait_ge(sem["ma%d" % i], 1)
        g.vector.tensor_scalar(sb[:, 0:H], pa[:, 0:H], 0.0, None, AluOpType.max).then_inc(sem["ra%d" % i], 1)
        g.scalar.wait_ge(sem["mb%d" % i], 1)
        g.scalar.activation(sb[:, H:D], pb[:, 0:H], ActivationFunctionType.Relu).then_inc(sem["rb%d" % i], 1)
        if need_v:
            g.tensor.wait_ge(sem["vrr%d" % (j % NS)], need_v)
        g.tensor.wait_ge(sem["ra%d" % i], 1)
        ma = g.tensor.matmul(T.oa[:, 0:H], blk[:, D:W], sb[:, 0:H], start=(i == 0), stop=(i == last))
        g.tensor.wait_ge(sem["rb%d" % i], 1)
        mb = g.tensor.matmul(T.ob[:, 0:H], blk[:, D:W], sb[:, H:D], start=(i == 0), stop=(i == last))
        if i == last:
            ma.then_inc(sem.fa, 1)
            mb.then_inc(sem.fb, 1)
    g.vector.wait_ge(sem.fa, 1)
    g.vector.tensor_copy(T.ys[:, 0:H], T.oa[:, 0:H]).then_inc(sem.cp, 1)
    g.scalar.wait_ge(sem.fb, 1)
    g.scalar.activation(T.ys[:, H:D], T.ob[:, 0:H], ActivationFunctionType.Copy).then_inc(sem.cp, 1)
    g.sync.wait_ge(sem.cp, 2)
    g.sync.dma_start(T.y[:, :], T.ys[:, :]).then_inc(sem.st, 16)
    g.sync.wait_ge(sem.st, 16)
